import numpy as np
import ml_dtypes


def mxq(x, axis, fmt="e4m3"):
    dtype, down = {"e4m3": (ml_dtypes.float8_e4m3fn, 7), "e5m2": (ml_dtypes.float8_e5m2, 14)}[fmt]
    v = np.moveaxis(np.asarray(x, np.float32).astype(ml_dtypes.bfloat16).astype(np.float64), axis, -1)
    blocks = v.reshape(v.shape[:-1] + (-1, 32))
    amax = np.abs(blocks).max(-1, keepdims=True)
    byte = np.maximum(np.where(amax > 0, np.frexp(amax)[1] - 1 + 127, 0) - down, 1)
    scale = np.exp2(byte - 127.0)
    codes = (blocks / scale).astype(np.float32).astype(dtype).astype(np.float64)
    return np.moveaxis((codes * scale).reshape(v.shape), -1, axis)


WIDE = False


def mx_kscale(k):
    if not WIDE:
        return np.ones(k)
    levels = np.array([10, -10, 5, -5, 0])
    if k % 512:
        return np.exp2(np.random.permutation(np.resize(levels, k // 32))).repeat(32)
    a = np.empty((k // 512, 16))
    for p in range(k // 512):
        a[p, :8] = np.random.permutation(np.resize(levels, 8))
        for g in range(8):
            far = levels[np.abs(levels - a[p, g]) >= 10]
            a[p, g + 8] = far[np.random.randint(len(far))]
    return np.exp2(a.ravel()).repeat(32)


def f64(x):
    return np.asarray(x).astype(np.float64)


def striped8(idx):
    return np.asarray(idx).reshape(8, -1, 16).transpose(0, 2, 1).reshape(128, -1).astype(np.uint16)


def unstriped8(offs):
    return offs.reshape(8, 16, -1).transpose(0, 2, 1).reshape(8, -1).astype(np.int64)


def pick8(x, idx, run):
    r = np.arange(len(x))
    return x[r[:, None], idx[r % (8 * run) // run]]


D, T, I, Q, X, E, M, C = 512, 2048, 512, 256, 32, 512, 512, 1024


def setup_inputs():
    n = np.random.standard_normal
    idx = np.stack([np.random.permutation(T)[:I] for _ in range(8)])
    fd = mx_kscale(D)
    fi = mx_kscale(I)
    fm = mx_kscale(M)
    ti = np.ones((8, T))
    np.put_along_axis(ti, idx, np.tile(fi, (8, 1)), axis=1)
    return {
        "query": (n((D, Q)) * (np.arange(D)[:, None] // 64 == np.arange(Q) % 8) * 0.0625 * fd[:, None]).astype(np.float32),
        "keys": (n((D, T)) / fd[:, None]).astype(np.float32),
        "skey": (n((D, M)) / fd[:, None]).astype(np.float32),
        "size": (np.random.uniform(0.5, 2.0, (1, I)) * fi).astype(np.float32),
        "ssz": (np.random.uniform(0.5, 2.0, (1, M)) * fm).astype(np.float32),
        "vals": (n((E, T)) / ti[np.arange(E) % 512 // 64]).astype(np.float32),
        "sval": (n((M, E)) / fm[:, None]).astype(np.float32),
        "own": ((np.arange(E)[:, None] // 64 == np.arange(Q) % 8) * 1.0).astype(np.float32),
        "offs": striped8(idx),
    }


def reference(query, keys, skey, size, ssz, vals, sval, own, offs):
    idx = unstriped8(offs)
    queryq = mxq(f64(query), 0, "e4m3")
    keysidxq = mxq(pick8(f64(keys), idx, 64), 0, "e4m3")
    a = queryq.T @ keysidxq
    skeyq = mxq(f64(skey), 0, "e4m3")
    b = queryq.T @ skeyq
    m1 = np.maximum(np.max(a, axis=1, keepdims=True), np.max(b, axis=1, keepdims=True))
    p = np.exp(a - m1)
    r = np.exp(b - m1)
    z = np.sum(p, axis=1, keepdims=True) + np.sum(r, axis=1, keepdims=True)
    w = p * f64(size) / z
    u = r * f64(ssz) / z
    wt = w.T
    ut = u.T
    vt = pick8(f64(vals), idx, 64).T
    vtq = mxq(vt, 0, "e4m3")
    wtq = mxq(wt, 0, "e4m3")
    svalq = mxq(f64(sval), 0, "e4m3")
    utq = mxq(ut, 0, "e4m3")
    o = vtq.T @ wtq + svalq.T @ utq
    ob = o * f64(own)
    y = ob.reshape(E, X, Q // X).sum(axis=2)
    return y

@@ -1,0 +1,237 @@
+from contextlib import ExitStack
+
+import concourse.mybir as mybir
+from concourse.masks import make_identity
+
+F32 = mybir.dt.float32
+BF16 = mybir.dt.bfloat16
+U32 = mybir.dt.uint32
+U16 = mybir.dt.uint16
+U8 = mybir.dt.uint8
+FP8X4 = mybir.dt.float8_e4m3fn_x4
+ALU = mybir.AluOpType
+EXP = mybir.ActivationFunctionType.Exp
+IDENTITY = mybir.ActivationFunctionType.Identity
+COPY = mybir.ActivationFunctionType.Copy
+AXIS_X = mybir.AxisListType.X
+
+P = 128
+PACK = 4
+POOL = 2048
+SLOTS = 512
+QUERIES = 256
+PLACES = 32
+HEADS = 8
+KEY_SPLIT = 336
+FLOPS = 4 * 2 * 512 * 512 * 256
+
+
+def tile_attend_ownlists_sinks_kernel(tc, query, keys, skey, size, ssz, vals, sval, own, offs, out):
+    nc = tc.nc
+    with ExitStack() as ctx:
+        sb = ctx.enter_context(tc.tile_pool(name="sb", bufs=1))
+        ps = ctx.enter_context(tc.psum_pool(name="ps", bufs=1))
+
+        def tile(name, shape, dtype):
+            return sb.tile(shape, dtype, name=name, align_bytes=64)
+
+        def load(name, shape, src):
+            dst = tile(name, shape, F32)
+            nc.sync.dma_start(out=dst[:], in_=src)
+            return dst
+
+        def quantise(codes, scales, grouped):
+            nc.vector.quantize_mx(out=codes.bitcast(FP8X4), scales=scales, in_=grouped)
+
+        def product(acc, lhs, rhs, start, stop):
+            nc.tensor.matmul_mx(out=acc, lhsT=lhs[0].bitcast(FP8X4), lhsT_scale=lhs[1],
+                                rhs=rhs[0].bitcast(FP8X4), rhs_scale=rhs[1], start=start, stop=stop)
+
+        def interleave(copy, dst, src):
+            copy(out=dst.rearrange("p (c i) t -> p c t i", i=4), in_=src.rearrange("p t (c i) -> p c t i", i=4))
+
+        def rows_4p(src):
+            return src.rearrange("(p t) n -> p t n", t=PACK)
+
+        def reuse(tag, name, shape, dtype):
+            return sb.tile(shape, dtype, name=name, tag=tag, align_bytes=64)
+
+        def mx_pair(name, width):
+            return (tile(name + "_codes", [P, width], U32), tile(name + "_scales", [P, width], U8))
+
+        def columns(pair, start, stop):
+            return (pair[0][:, start:stop], pair[1][:, start:stop])
+
+        offsets = sb.tile([P, SLOTS // 16], U16, name="offsets")
+        sk_raw = load("sk_raw", [P, PACK, SLOTS], rows_4p(skey))
+        q_raw = load("q_raw", [P, PACK, QUERIES], rows_4p(query))
+        ssz_col = load("ssz_col", [P, PACK], ssz.rearrange("o (p c) -> (o p) c", c=PACK))
+        nc.sync.dma_start(offsets[:], offs)
+        size_col = load("size_col", [P, PACK], size.rearrange("o (p c) -> (o p) c", c=PACK))
+        key_pool = [load("key_pool%d" % t, [P, POOL], rows_4p(keys)[:, t, :]) for t in range(PACK)]
+        val_pool = [load("val_pool0", [P, POOL], rows_4p(vals)[:, 0, :])]
+        sv_raw = load("sv_raw", [P, PACK, SLOTS], rows_4p(sval))
+        for t in range(1, PACK):
+            val_pool.append(load("val_pool%d" % t, [P, POOL], rows_4p(vals)[:, t, :]))
+        own_sb = load("own_sb", [P, PACK, QUERIES], rows_4p(own))
+
+        ident = tile("ident", [P, P], F32)
+        make_identity(nc, ident[:])
+        warm_in = tile("warm_in", [P, 1], F32)
+        warm_out = tile("warm_out", [P, 1], F32)
+        nc.vector.memset(warm_in[:], 0.0)
+        nc.scalar.activation(out=warm_out[:], in_=warm_in[:], func=EXP)
+
+        sk_grouped = tile("sk_grouped", [P, SLOTS, PACK], BF16)
+        interleave(nc.vector.tensor_copy, sk_grouped[:, 0:KEY_SPLIT, :], sk_raw[:, :, 0:KEY_SPLIT])
+        interleave(nc.scalar.copy, sk_grouped[:, KEY_SPLIT:, :], sk_raw[:, :, KEY_SPLIT:])
+        q_grouped = tile("q_grouped", [P, QUERIES, PACK], BF16)
+        interleave(nc.vector.tensor_copy, q_grouped[:], q_raw[:])
+        sk_mx = mx_pair("sk", SLOTS)
+        quantise(sk_mx[0][:], sk_mx[1][:], sk_grouped[:].rearrange("p n t -> p (n t)"))
+        q_mx = mx_pair("q", QUERIES)
+        quantise(q_mx[0][:], q_mx[1][:], q_grouped[:].rearrange("p n t -> p (n t)"))
+
+        def spread(name, col):
+            bank = ps.tile([P, PACK, P], F32, name="bank_" + name, tag="turn", bufs=4)
+            for c in range(PACK):
+                nc.tensor.transpose(bank[:, c, :], col[:, c:c + 1].to_broadcast([P, P]), ident[:])
+            row = tile(name, [P, P, PACK], F32)
+            nc.scalar.copy(out=row[:], in_=bank[:].rearrange("p c n -> p n c"))
+            return row[:].rearrange("p n c -> p (n c)")
+
+        def scores(name, j, keys_mx, tag):
+            bank = ps.tile([P, SLOTS], F32, name=name, tag=tag)
+            product(bank[:], columns(q_mx, j * P, (j + 1) * P), columns(keys_mx, 0, SLOTS), True, True)
+            return bank
+
+        ssz_all = spread("ssz_all", ssz_col)
+        size_all = spread("size_all", size_col)
+        key_planes = tile("key_planes", [P, PACK, SLOTS], BF16)
+
+        def gather_keys(t):
+            nc.vector.tensor_copy(out=key_planes[:, t, :], in_=key_pool[t][:].indirect(offsets[:]))
+
+        gather_keys(0)
+        neg_max_b = reuse("key_pool0", "neg_max_b", [P, 2], F32)
+        sum_b = tile("sum_b", [P, 2], F32)
+        exp_b = []
+        for j in range(2):
+            score = scores("score_b%d" % j, j, sk_mx, "acc%d" % j)
+            nc.vector.tensor_reduce(out=neg_max_b[:, j:j + 1], in_=score[:], axis=AXIS_X, op=ALU.max, negate=True)
+            exp_b.append(tile("exp_b%d" % j, [P, SLOTS], F32))
+            nc.scalar.activation(out=exp_b[j][:], in_=score[:], func=EXP, bias=neg_max_b[:, j:j + 1],
+                                 accum_out=sum_b[:, j:j + 1])
+        gather_keys(1)
+        weighted_b = reuse("key_pool1", "weighted_b", [P, 2, SLOTS], F32)
+        for j in range(2):
+            nc.vector.tensor_tensor(out=weighted_b[:, j, :], in0=exp_b[j][:], in1=ssz_all, op=ALU.mult)
+        gather_keys(2)
+        gather_keys(3)
+
+        key_grouped = tile("key_grouped", [P, SLOTS, PACK], BF16)
+        interleave(nc.vector.tensor_copy, key_grouped[:, 0:KEY_SPLIT, :], key_planes[:, :, 0:KEY_SPLIT])
+        interleave(nc.scalar.copy, key_grouped[:, KEY_SPLIT:, :], key_planes[:, :, KEY_SPLIT:])
+        key_mx = mx_pair("key", SLOTS)
+        quantise(key_mx[0][:], key_mx[1][:], key_grouped[:].rearrange("p n t -> p (n t)"))
+
+        def turn(bank, rows):
+            words = rows.bitcast(F32)
+            for u in range(2):
+                nc.tensor.transpose(bank[:, u, :], words[:, u::2], ident[:])
+
+        val_picked = [tile("val_picked%d" % t, [P, SLOTS], BF16) for t in range(PACK)]
+        val_grouped = [tile("val_grouped01", [P, 2, SLOTS], BF16), tile("val_grouped2", [P, 1, SLOTS], BF16),
+                       tile("val_grouped3", [P, 1, SLOTS], BF16)]
+
+        def gather_values(t):
+            nc.vector.tensor_copy(out=val_picked[t][:], in_=val_pool[t][:].indirect(offsets[:]))
+
+        def turn_values(t):
+            bank = ps.tile([P, 2, P], F32, name="bank_val%d" % t, tag="turn", bufs=4)
+            turn(bank[:], val_picked[t][:])
+            grouped = val_grouped[max(t - 1, 0)][:, t if t < 2 else 0, :]
+            nc.scalar.copy(out=grouped.bitcast(F32).rearrange("p (n u) -> p n u", u=2),
+                           in_=bank[:].rearrange("p u n -> p n u"))
+
+        def quantise_values(first, last):
+            codes, scales = columns(val_mx, first * P, last * P)
+            quantise(codes, scales, val_grouped[last - 2][:].rearrange("p t n -> p (t n)"))
+
+        sv_grouped = tile("sv_grouped", [P, PACK, P, PACK], BF16)
+
+        def cast_sink_values(part):
+            s = slice(part * 32, (part + 1) * 32)
+            nc.scalar.copy(out=sv_grouped[:].rearrange("p t s j -> p s j t")[:, s],
+                           in_=sv_raw[:].rearrange("p j (s t) -> p s j t", t=PACK)[:, s])
+
+        gather_values(0)
+        turn_values(0)
+        cast_sink_values(0)
+        neg_max = tile("neg_max", [P, 2], F32)
+        sum_a = tile("sum_a", [P, 2], F32)
+        shift = tile("shift", [P, 2], F32)
+        total = tile("total", [P, 2], F32)
+        exp_a = []
+        neg_a = reuse("val_pool0", "neg_a", [P, 2, SLOTS], F32)
+        for j in range(2):
+            score = scores("score_a%d" % j, j, key_mx, "acc%d" % (2 + j))
+            nc.vector.tensor_scalar(out=neg_a[:, j, :], in0=score[:], scalar1=-1.0, scalar2=neg_max_b[:, j:j + 1],
+                                    op0=ALU.mult, op1=ALU.min, accum_out=neg_max[:, j:j + 1])
+            exp_a.append(tile("exp_a%d" % j, [P, SLOTS], F32))
+            nc.scalar.activation(out=exp_a[j][:], in_=neg_a[:, j, :], func=EXP, scale=-1.0, bias=neg_max[:, j:j + 1],
+                                 accum_out=sum_a[:, j:j + 1])
+            nc.scalar.activation(out=shift[:, j:j + 1], in_=neg_max_b[:, j:j + 1], func=EXP, scale=-1.0,
+                                 bias=neg_max[:, j:j + 1])
+        for j in range(2):
+            nc.scalar.activation(out=total[:, j:j + 1], in_=sum_b[:, j:j + 1], func=IDENTITY,
+                                 scale=shift[:, j:j + 1], bias=sum_a[:, j:j + 1])
+        gather_values(1)
+        inverse = reuse("val_pool1", "inverse", [P, 2], F32)
+        nc.vector.reciprocal(out=inverse[:], in_=total[:])
+        for part in range(1, 4):
+            cast_sink_values(part)
+        factor_b = tile("factor_b", [P, 2], F32)
+        for j in range(2):
+            nc.scalar.activation(out=factor_b[:, j:j + 1], in_=shift[:, j:j + 1], func=COPY, scale=inverse[:, j:j + 1])
+        w_rows = [[tile("w_rows%d%d" % (a, j), [P, SLOTS], BF16) for j in range(2)] for a in range(2)]
+        for j in range(2):
+            nc.vector.scalar_tensor_tensor(out=w_rows[0][j][:], in0=exp_a[j][:], scalar=inverse[:, j:j + 1],
+                                           in1=size_all, op0=ALU.mult, op1=ALU.mult)
+            nc.scalar.activation(out=w_rows[1][j][:], in_=weighted_b[:, j, :], func=COPY, scale=factor_b[:, j:j + 1])
+        gather_values(2)
+        turn_values(1)
+        w_grouped = [tile("w_grouped%d" % a, [P, QUERIES * PACK], BF16) for a in range(2)]
+        for a in (1, 0):
+            bank = ps.tile([P, 2, 2, P], F32, name="bank_w%d" % a, tag="turn", bufs=4)
+            for j in range(2):
+                turn(bank[:, j], w_rows[a][j][:])
+            nc.scalar.copy(out=w_grouped[a][:].bitcast(F32).rearrange("p (j n u) -> p j n u", j=2, u=2),
+                           in_=bank[:].rearrange("p j u n -> p j n u"))
+        turn_values(2)
+        sv_mx = (reuse("val_pool2", "sv_codes", [P, SLOTS], U32), tile("sv_scales", [P, SLOTS], U8))
+        quantise(sv_mx[0][:], sv_mx[1][:], sv_grouped[:].rearrange("p t s j -> p (t s j)"))
+        gather_values(3)
+        turn_values(3)
+        late_codes = reuse("val_pool3", "late_codes", [P, 2 * SLOTS], U32)
+        val_mx = (late_codes[:, 0:SLOTS], tile("val_scales", [P, SLOTS], U8))
+        w_mx = [(late_codes[:, SLOTS + a * QUERIES:SLOTS + (a + 1) * QUERIES], tile("w_scales%d" % a, [P, QUERIES], U8))
+                for a in range(2)]
+        quantise(w_mx[1][0][:], w_mx[1][1][:], w_grouped[1][:])
+        quantise_values(0, 2)
+        quantise(w_mx[0][0][:], w_mx[0][1][:], w_grouped[0][:])
+        quantise_values(2, 3)
+        quantise_values(3, 4)
+
+        result = tile("result", [P, PACK, PLACES], F32)
+        masked = tile("masked", [P, PACK, QUERIES], F32)
+        for t in range(PACK):
+            acc = ps.tile([P, QUERIES], F32, name="acc_o%d" % t, tag="acc%d" % t)
+            product(acc[:], columns(sv_mx, t * P, (t + 1) * P), columns(w_mx[1], 0, QUERIES), True, False)
+            product(acc[:], columns(val_mx, t * P, (t + 1) * P), columns(w_mx[0], 0, QUERIES), False, True)
+            nc.vector.tensor_tensor(out=masked[:, t, :], in0=acc[:], in1=own_sb[:, t, :], op=ALU.mult)
+        for first, last in ((0, 3), (3, 4)):
+            nc.vector.tensor_reduce(out=result[:, first:last, :],
+                                    in_=masked[:, first:last, :].rearrange("p t (x h) -> p t x h", h=HEADS),
+                                    axis=AXIS_X, op=ALU.add)
+        nc.sync.dma_start(out=rows_4p(out), in_=result[:])

@@ -22,7 +22,9 @@ SLOTS = 512
 QUERIES = 256
 PLACES = 32
 HEADS = 8
-KEY_SPLIT = 336
+KEY_SPLIT = 84
+REGION = 8192
+REGIONS = ("key3", "val1", "val2", "val3", "small")
 FLOPS = 4 * 2 * 512 * 512 * 256
 
 
@@ -30,18 +32,21 @@ def tile_attend_ownlists_sinks_kernel(tc, query, keys, skey, size, ssz, vals, sv
     nc = tc.nc
     with ExitStack() as ctx:
         sb = ctx.enter_context(tc.tile_pool(name="sb", bufs=1))
+        shared = ctx.enter_context(tc.tile_pool(name="shared", bufs=1))
         ps = ctx.enter_context(tc.psum_pool(name="ps", bufs=1))
 
         def tile(name, shape, dtype):
             return sb.tile(shape, dtype, name=name, align_bytes=64)
 
-        def load(name, shape, src):
-            dst = tile(name, shape, F32)
+        def placed(region, start, name, shape, dtype):
+            return shared.tile(shape, dtype, name=name, align_bytes=64, offset=REGIONS.index(region) * REGION + start)
+
+        def load(dst, src):
             nc.sync.dma_start(out=dst[:], in_=src)
             return dst
 
-        def quantise(codes, scales, grouped):
-            nc.vector.quantize_mx(out=codes.bitcast(FP8X4), scales=scales, in_=grouped)
+        def quantise(pair, grouped):
+            nc.vector.quantize_mx(out=pair[0].bitcast(FP8X4), scales=pair[1], in_=grouped)
 
         def product(acc, lhs, rhs, start, stop):
             nc.tensor.matmul_mx(out=acc, lhsT=lhs[0].bitcast(FP8X4), lhsT_scale=lhs[1],
@@ -50,188 +55,190 @@ def tile_attend_ownlists_sinks_kernel(tc, query, keys, skey, size, ssz, vals, sv
         def interleave(copy, dst, src):
             copy(out=dst.rearrange("p (c i) t -> p c t i", i=4), in_=src.rearrange("p t (c i) -> p c t i", i=4))
 
+        def deal(copy, dst, src, places):
+            copy(out=dst.rearrange("p (u s e) t -> p s t u e", u=2, e=2)[:, places],
+                 in_=src.rearrange("p t (s u e) -> p s t u e", u=2, e=2)[:, places])
+
         def rows_4p(src):
             return src.rearrange("(p t) n -> p t n", t=PACK)
-
-        def reuse(tag, name, shape, dtype):
-            return sb.tile(shape, dtype, name=name, tag=tag, align_bytes=64)
-
-        def mx_pair(name, width):
-            return (tile(name + "_codes", [P, width], U32), tile(name + "_scales", [P, width], U8))
 
         def columns(pair, start, stop):
             return (pair[0][:, start:stop], pair[1][:, start:stop])
 
+        def mx_pair(name, width, region=None, start=0):
+            codes = tile(name + "_codes", [P, width], U32) if region is None else placed(
+                region, start, name + "_codes", [P, width], U32)
+            return (codes[:], tile(name + "_scales", [P, width], U8)[:])
+
         offsets = sb.tile([P, SLOTS // 16], U16, name="offsets")
-        sk_raw = load("sk_raw", [P, PACK, SLOTS], rows_4p(skey))
-        q_raw = load("q_raw", [P, PACK, QUERIES], rows_4p(query))
-        ssz_col = load("ssz_col", [P, PACK], ssz.rearrange("o (p c) -> (o p) c", c=PACK))
+        ssz_col = tile("ssz_col", [P, PACK], F32)
+        size_col = tile("size_col", [P, PACK], F32)
+        nc.scalar.dma_start(out=ssz_col[:], in_=ssz.rearrange("o (p c) -> (o p) c", c=PACK))
+        nc.scalar.dma_start(out=size_col[:], in_=size.rearrange("o (p c) -> (o p) c", c=PACK))
+        q_raw = load(tile("q_raw", [P, PACK, QUERIES], F32), rows_4p(query))
+        sk_raw = load(tile("sk_raw", [P, PACK, SLOTS], F32), rows_4p(skey))
         nc.sync.dma_start(offsets[:], offs)
-        size_col = load("size_col", [P, PACK], size.rearrange("o (p c) -> (o p) c", c=PACK))
-        key_pool = [load("key_pool%d" % t, [P, POOL], rows_4p(keys)[:, t, :]) for t in range(PACK)]
-        val_pool = [load("val_pool0", [P, POOL], rows_4p(vals)[:, 0, :])]
-        sv_raw = load("sv_raw", [P, PACK, SLOTS], rows_4p(sval))
+        key_pool = [load(tile("key_pool%d" % t, [P, POOL], F32), rows_4p(keys)[:, t, :]) for t in range(PACK - 1)]
+        key_pool.append(load(placed("key3", 0, "key_pool3", [P, POOL], F32), rows_4p(keys)[:, 3, :]))
+        val_pool = [load(tile("val_pool0", [P, POOL], F32), rows_4p(vals)[:, 0, :])]
+        sv_raw = load(tile("sv_raw", [P, PACK, SLOTS], F32), rows_4p(sval))
         for t in range(1, PACK):
-            val_pool.append(load("val_pool%d" % t, [P, POOL], rows_4p(vals)[:, t, :]))
-        own_sb = load("own_sb", [P, PACK, QUERIES], rows_4p(own))
+            val_pool.append(load(placed("val%d" % t, 0, "val_pool%d" % t, [P, POOL], F32), rows_4p(vals)[:, t, :]))
+        own_pairs = [load(tile("own_pair%d" % i, [P, 2, QUERIES], F32), rows_4p(own)[:, 2 * i:2 * i + 2, :])
+                     for i in range(2)]
 
         ident = tile("ident", [P, P], F32)
         make_identity(nc, ident[:])
-        warm_in = tile("warm_in", [P, 1], F32)
-        warm_out = tile("warm_out", [P, 1], F32)
-        nc.vector.memset(warm_in[:], 0.0)
-        nc.scalar.activation(out=warm_out[:], in_=warm_in[:], func=EXP)
 
-        sk_grouped = tile("sk_grouped", [P, SLOTS, PACK], BF16)
-        interleave(nc.vector.tensor_copy, sk_grouped[:, 0:KEY_SPLIT, :], sk_raw[:, :, 0:KEY_SPLIT])
-        interleave(nc.scalar.copy, sk_grouped[:, KEY_SPLIT:, :], sk_raw[:, :, KEY_SPLIT:])
+        def deal_on_both(dst, src):
+            deal(nc.vector.tensor_copy, dst, src, slice(0, KEY_SPLIT))
+            deal(nc.scalar.copy, dst, src, slice(KEY_SPLIT, P))
+
         q_grouped = tile("q_grouped", [P, QUERIES, PACK], BF16)
         interleave(nc.vector.tensor_copy, q_grouped[:], q_raw[:])
-        sk_mx = mx_pair("sk", SLOTS)
-        quantise(sk_mx[0][:], sk_mx[1][:], sk_grouped[:].rearrange("p n t -> p (n t)"))
         q_mx = mx_pair("q", QUERIES)
-        quantise(q_mx[0][:], q_mx[1][:], q_grouped[:].rearrange("p n t -> p (n t)"))
+        quantise(q_mx, q_grouped[:].rearrange("p n t -> p (n t)"))
+        sk_grouped = tile("sk_grouped", [P, SLOTS, PACK], BF16)
+        deal_on_both(sk_grouped[:], sk_raw[:])
+        sk_mx = mx_pair("sk", SLOTS)
+        quantise(sk_mx, sk_grouped[:].rearrange("p n t -> p (n t)"))
 
         def spread(name, col):
             bank = ps.tile([P, PACK, P], F32, name="bank_" + name, tag="turn", bufs=4)
             for c in range(PACK):
                 nc.tensor.transpose(bank[:, c, :], col[:, c:c + 1].to_broadcast([P, P]), ident[:])
-            row = tile(name, [P, P, PACK], F32)
-            nc.scalar.copy(out=row[:], in_=bank[:].rearrange("p c n -> p n c"))
-            return row[:].rearrange("p n c -> p (n c)")
+            row = tile(name, [P, SLOTS], F32)
+            nc.scalar.copy(out=row[:].rearrange("p (u s e) -> p u s e", u=2, e=2),
+                           in_=bank[:].rearrange("p (u e) s -> p u s e", u=2))
+            return row[:]
 
         def scores(name, j, keys_mx, tag):
             bank = ps.tile([P, SLOTS], F32, name=name, tag=tag)
-            product(bank[:], columns(q_mx, j * P, (j + 1) * P), columns(keys_mx, 0, SLOTS), True, True)
+            product(bank[:], columns(q_mx, j * P, (j + 1) * P), keys_mx, True, True)
             return bank
 
-        ssz_all = spread("ssz_all", ssz_col)
-        size_all = spread("size_all", size_col)
         key_planes = tile("key_planes", [P, PACK, SLOTS], BF16)
-
-        def gather_keys(t):
+        for t in range(PACK):
             nc.vector.tensor_copy(out=key_planes[:, t, :], in_=key_pool[t][:].indirect(offsets[:]))
 
-        gather_keys(0)
-        neg_max_b = reuse("key_pool0", "neg_max_b", [P, 2], F32)
+        neg_max_b = tile("neg_max_b", [P, 2], F32)
         sum_b = tile("sum_b", [P, 2], F32)
-        exp_b = []
+        exp_b = tile("exp_b", [P, 2, SLOTS], F32)
         for j in range(2):
             score = scores("score_b%d" % j, j, sk_mx, "acc%d" % j)
             nc.vector.tensor_reduce(out=neg_max_b[:, j:j + 1], in_=score[:], axis=AXIS_X, op=ALU.max, negate=True)
-            exp_b.append(tile("exp_b%d" % j, [P, SLOTS], F32))
-            nc.scalar.activation(out=exp_b[j][:], in_=score[:], func=EXP, bias=neg_max_b[:, j:j + 1],
+            nc.scalar.activation(out=exp_b[:, j, :], in_=score[:], func=EXP, bias=neg_max_b[:, j:j + 1],
                                  accum_out=sum_b[:, j:j + 1])
-        gather_keys(1)
-        weighted_b = reuse("key_pool1", "weighted_b", [P, 2, SLOTS], F32)
-        for j in range(2):
-            nc.vector.tensor_tensor(out=weighted_b[:, j, :], in0=exp_b[j][:], in1=ssz_all, op=ALU.mult)
-        gather_keys(2)
-        gather_keys(3)
+        ssz_all = spread("ssz_all", ssz_col)
+        size_all = spread("size_all", size_col)
 
         key_grouped = tile("key_grouped", [P, SLOTS, PACK], BF16)
-        interleave(nc.vector.tensor_copy, key_grouped[:, 0:KEY_SPLIT, :], key_planes[:, :, 0:KEY_SPLIT])
-        interleave(nc.scalar.copy, key_grouped[:, KEY_SPLIT:, :], key_planes[:, :, KEY_SPLIT:])
-        key_mx = mx_pair("key", SLOTS)
-        quantise(key_mx[0][:], key_mx[1][:], key_grouped[:].rearrange("p n t -> p (n t)"))
-
-        def turn(bank, rows):
-            words = rows.bitcast(F32)
-            for u in range(2):
-                nc.tensor.transpose(bank[:, u, :], words[:, u::2], ident[:])
+        deal_on_both(key_grouped[:], key_planes[:])
+        key_mx = (tile("key_codes", [P, SLOTS], U32)[:], placed("small", 0, "key_scales", [P, SLOTS], U8)[:])
+        quantise(key_mx, key_grouped[:].rearrange("p n t -> p (n t)"))
+        weighted_b = [placed("key3", 0, "weighted_b0", [P, SLOTS], F32)]
+        nc.vector.tensor_tensor(out=weighted_b[0][:], in0=exp_b[:, 0, :], in1=ssz_all, op=ALU.mult)
 
         val_picked = [tile("val_picked%d" % t, [P, SLOTS], BF16) for t in range(PACK)]
-        val_grouped = [tile("val_grouped01", [P, 2, SLOTS], BF16), tile("val_grouped2", [P, 1, SLOTS], BF16),
-                       tile("val_grouped3", [P, 1, SLOTS], BF16)]
 
         def gather_values(t):
             nc.vector.tensor_copy(out=val_picked[t][:], in_=val_pool[t][:].indirect(offsets[:]))
 
-        def turn_values(t):
+        def turn_values(t, grouped):
             bank = ps.tile([P, 2, P], F32, name="bank_val%d" % t, tag="turn", bufs=4)
-            turn(bank[:], val_picked[t][:])
-            grouped = val_grouped[max(t - 1, 0)][:, t if t < 2 else 0, :]
+            words = val_picked[t][:].bitcast(F32)
+            for u in range(2):
+                nc.tensor.transpose(bank[:, u, :], words[:, u::2], ident[:])
             nc.scalar.copy(out=grouped.bitcast(F32).rearrange("p (n u) -> p n u", u=2),
                            in_=bank[:].rearrange("p u n -> p n u"))
 
-        def quantise_values(first, last):
-            codes, scales = columns(val_mx, first * P, last * P)
-            quantise(codes, scales, val_grouped[last - 2][:].rearrange("p t n -> p (t n)"))
-
-        sv_grouped = tile("sv_grouped", [P, PACK, P, PACK], BF16)
-
-        def cast_sink_values(part):
-            s = slice(part * 32, (part + 1) * 32)
-            nc.scalar.copy(out=sv_grouped[:].rearrange("p t s j -> p s j t")[:, s],
-                           in_=sv_raw[:].rearrange("p j (s t) -> p s j t", t=PACK)[:, s])
-
         gather_values(0)
-        turn_values(0)
-        cast_sink_values(0)
+        neg_a = tile("neg_a", [P, 2, SLOTS], F32)
         neg_max = tile("neg_max", [P, 2], F32)
         sum_a = tile("sum_a", [P, 2], F32)
+        total = placed("small", 2048, "total", [P, 2], F32)
+        exp_a = tile("exp_a", [P, 2, SLOTS], F32)
         shift = tile("shift", [P, 2], F32)
-        total = tile("total", [P, 2], F32)
-        exp_a = []
-        neg_a = reuse("val_pool0", "neg_a", [P, 2, SLOTS], F32)
         for j in range(2):
             score = scores("score_a%d" % j, j, key_mx, "acc%d" % (2 + j))
             nc.vector.tensor_scalar(out=neg_a[:, j, :], in0=score[:], scalar1=-1.0, scalar2=neg_max_b[:, j:j + 1],
                                     op0=ALU.mult, op1=ALU.min, accum_out=neg_max[:, j:j + 1])
-            exp_a.append(tile("exp_a%d" % j, [P, SLOTS], F32))
-            nc.scalar.activation(out=exp_a[j][:], in_=neg_a[:, j, :], func=EXP, scale=-1.0, bias=neg_max[:, j:j + 1],
-                                 accum_out=sum_a[:, j:j + 1])
             nc.scalar.activation(out=shift[:, j:j + 1], in_=neg_max_b[:, j:j + 1], func=EXP, scale=-1.0,
                                  bias=neg_max[:, j:j + 1])
+            nc.scalar.activation(out=exp_a[:, j, :], in_=neg_a[:, j, :], func=EXP, scale=-1.0,
+                                 bias=neg_max[:, j:j + 1], accum_out=sum_a[:, j:j + 1])
         for j in range(2):
             nc.scalar.activation(out=total[:, j:j + 1], in_=sum_b[:, j:j + 1], func=IDENTITY,
                                  scale=shift[:, j:j + 1], bias=sum_a[:, j:j + 1])
+        weighted_b.append(placed("small", 0, "weighted_b1", [P, SLOTS], F32))
+        nc.vector.tensor_tensor(out=weighted_b[1][:], in0=exp_b[:, 1, :], in1=ssz_all, op=ALU.mult)
+
+        def cast_sink_values(copy, grouped, pair, s):
+            copy(out=grouped[:].rearrange("p t s j -> p s j t")[:, s],
+                 in_=sv_raw[:].rearrange("p j (s t) -> p s j t", t=PACK)[:, s, :, 2 * pair:2 * pair + 2])
+
+        sv_grouped = [tile("sv_grouped0", [P, 2, P, PACK], BF16)]
+
         gather_values(1)
-        inverse = reuse("val_pool1", "inverse", [P, 2], F32)
+        inverse = placed("val1", 0, "inverse", [P, 2], F32)
         nc.vector.reciprocal(out=inverse[:], in_=total[:])
-        for part in range(1, 4):
-            cast_sink_values(part)
         factor_b = tile("factor_b", [P, 2], F32)
         for j in range(2):
             nc.scalar.activation(out=factor_b[:, j:j + 1], in_=shift[:, j:j + 1], func=COPY, scale=inverse[:, j:j + 1])
-        w_rows = [[tile("w_rows%d%d" % (a, j), [P, SLOTS], BF16) for j in range(2)] for a in range(2)]
+        w_rows = [placed("small", 4096 + 2048 * a, "w_rows%d" % a, [P, 2, SLOTS], BF16) for a in range(2)]
         for j in range(2):
-            nc.vector.scalar_tensor_tensor(out=w_rows[0][j][:], in0=exp_a[j][:], scalar=inverse[:, j:j + 1],
+            nc.vector.scalar_tensor_tensor(out=w_rows[0][:, j, :], in0=exp_a[:, j, :], scalar=inverse[:, j:j + 1],
                                            in1=size_all, op0=ALU.mult, op1=ALU.mult)
-            nc.scalar.activation(out=w_rows[1][j][:], in_=weighted_b[:, j, :], func=COPY, scale=factor_b[:, j:j + 1])
+            nc.scalar.activation(out=w_rows[1][:, j, :], in_=weighted_b[j][:], func=COPY, scale=factor_b[:, j:j + 1])
         gather_values(2)
-        turn_values(1)
+        grouped01 = placed("small", 2048, "val_grouped01", [P, 2, SLOTS], BF16)
+        val_grouped = [tile("val_grouped%d" % t, [P, SLOTS], BF16) for t in range(2, PACK)]
+        for t in range(2):
+            turn_values(t, grouped01[:, t, :])
         w_grouped = [tile("w_grouped%d" % a, [P, QUERIES * PACK], BF16) for a in range(2)]
-        for a in (1, 0):
+        for a in range(2):
             bank = ps.tile([P, 2, 2, P], F32, name="bank_w%d" % a, tag="turn", bufs=4)
+            words = w_rows[a][:].bitcast(F32)
             for j in range(2):
-                turn(bank[:, j], w_rows[a][j][:])
+                for u in range(2):
+                    nc.tensor.transpose(bank[:, j, u, :], words[:, j, u * P:(u + 1) * P], ident[:])
             nc.scalar.copy(out=w_grouped[a][:].bitcast(F32).rearrange("p (j n u) -> p j n u", j=2, u=2),
                            in_=bank[:].rearrange("p j u n -> p j n u"))
-        turn_values(2)
-        sv_mx = (reuse("val_pool2", "sv_codes", [P, SLOTS], U32), tile("sv_scales", [P, SLOTS], U8))
-        quantise(sv_mx[0][:], sv_mx[1][:], sv_grouped[:].rearrange("p t s j -> p (t s j)"))
+        for half in range(2):
+            cast_sink_values(nc.scalar.copy, sv_grouped[0], 0, slice(64 * half, 64 * half + 64))
+        turn_values(2, val_grouped[0][:])
         gather_values(3)
-        turn_values(3)
-        late_codes = reuse("val_pool3", "late_codes", [P, 2 * SLOTS], U32)
-        val_mx = (late_codes[:, 0:SLOTS], tile("val_scales", [P, SLOTS], U8))
-        w_mx = [(late_codes[:, SLOTS + a * QUERIES:SLOTS + (a + 1) * QUERIES], tile("w_scales%d" % a, [P, QUERIES], U8))
-                for a in range(2)]
-        quantise(w_mx[1][0][:], w_mx[1][1][:], w_grouped[1][:])
-        quantise_values(0, 2)
-        quantise(w_mx[0][0][:], w_mx[0][1][:], w_grouped[0][:])
-        quantise_values(2, 3)
-        quantise_values(3, 4)
+        turn_values(3, val_grouped[1][:])
+        sv_grouped.append(placed("small", 6144, "sv_grouped1", [P, 2, P, PACK], BF16))
+        for half in range(2):
+            cast_sink_values(nc.scalar.copy, sv_grouped[1], 1, slice(64 * half, 64 * half + 64))
+
+        mx01 = mx_pair("val01", 2 * P, "val3", 0)
+        w_mx = [mx_pair("w0", QUERIES, "val3", 1024), mx_pair("w1", QUERIES, "val3", 2048)]
+        sv_mx = [mx_pair("sv%d" % i, 2 * P, "val3", 3072 + 1024 * i) for i in range(2)]
+        val_mx = [columns(mx01, 0, P), columns(mx01, P, 2 * P), mx_pair("val2", P, "val3", 5120), mx_pair("val3", P)]
+        quantise(mx01, grouped01[:].rearrange("p t n -> p (t n)"))
+        quantise(w_mx[0], w_grouped[0][:])
+        quantise(sv_mx[0], sv_grouped[0][:].rearrange("p t s j -> p (t s j)"))
+        quantise(w_mx[1], w_grouped[1][:])
+        for t in range(2, PACK):
+            quantise(val_mx[t], val_grouped[t - 2][:])
+        quantise(sv_mx[1], sv_grouped[1][:].rearrange("p t s j -> p (t s j)"))
 
         result = tile("result", [P, PACK, PLACES], F32)
         masked = tile("masked", [P, PACK, QUERIES], F32)
+        acc = [ps.tile([P, QUERIES], F32, name="acc_o%d" % t, tag="acc%d" % t) for t in range(PACK)]
+        for t in range(2):
+            product(acc[t][:], val_mx[t], w_mx[0], True, False)
         for t in range(PACK):
-            acc = ps.tile([P, QUERIES], F32, name="acc_o%d" % t, tag="acc%d" % t)
-            product(acc[:], columns(sv_mx, t * P, (t + 1) * P), columns(w_mx[1], 0, QUERIES), True, False)
-            product(acc[:], columns(val_mx, t * P, (t + 1) * P), columns(w_mx[0], 0, QUERIES), False, True)
-            nc.vector.tensor_tensor(out=masked[:, t, :], in0=acc[:], in1=own_sb[:, t, :], op=ALU.mult)
-        for first, last in ((0, 3), (3, 4)):
-            nc.vector.tensor_reduce(out=result[:, first:last, :],
-                                    in_=masked[:, first:last, :].rearrange("p t (x h) -> p t x h", h=HEADS),
-                                    axis=AXIS_X, op=ALU.add)
+            if t >= 2:
+                product(acc[t][:], val_mx[t], w_mx[0], True, False)
+            product(acc[t][:], columns(sv_mx[t // 2], t % 2 * P, (t % 2 + 1) * P), w_mx[1], False, True)
+        for pair in range(2):
+            for t in (2 * pair, 2 * pair + 1):
+                nc.vector.tensor_tensor(out=masked[:, t, :], in0=acc[t][:], in1=own_pairs[pair][:, t % 2, :],
+                                        op=ALU.mult)
+            for t in (2 * pair, 2 * pair + 1):
+                nc.vector.tensor_reduce(out=result[:, t, :], in_=masked[:, t, :].rearrange("p (x h) -> p x h", h=HEADS),
+                                        axis=AXIS_X, op=ALU.add)
         nc.sync.dma_start(out=rows_4p(out), in_=result[:])

@@ -24,7 +24,7 @@ PLACES = 32
 HEADS = 8
 KEY_SPLIT = 84
 REGION = 8192
-REGIONS = ("key3", "val1", "val2", "val3", "small")
+REGIONS = ("val0", "val2", "val3", "total", "picked2")
 FLOPS = 4 * 2 * 512 * 512 * 256
 
 
@@ -78,11 +78,11 @@ def tile_attend_ownlists_sinks_kernel(tc, query, keys, skey, size, ssz, vals, sv
         q_raw = load(tile("q_raw", [P, PACK, QUERIES], F32), rows_4p(query))
         sk_raw = load(tile("sk_raw", [P, PACK, SLOTS], F32), rows_4p(skey))
         nc.sync.dma_start(offsets[:], offs)
-        key_pool = [load(tile("key_pool%d" % t, [P, POOL], F32), rows_4p(keys)[:, t, :]) for t in range(PACK - 1)]
-        key_pool.append(load(placed("key3", 0, "key_pool3", [P, POOL], F32), rows_4p(keys)[:, 3, :]))
-        val_pool = [load(tile("val_pool0", [P, POOL], F32), rows_4p(vals)[:, 0, :])]
+        key_pool = [load(tile("key_pool%d" % t, [P, POOL], F32), rows_4p(keys)[:, t, :]) for t in range(PACK)]
+        val_pool = [load(placed("val0", 0, "val_pool0", [P, POOL], F32), rows_4p(vals)[:, 0, :]),
+                    load(tile("val_pool1", [P, POOL], F32), rows_4p(vals)[:, 1, :])]
         sv_raw = load(tile("sv_raw", [P, PACK, SLOTS], F32), rows_4p(sval))
-        for t in range(1, PACK):
+        for t in range(2, PACK):
             val_pool.append(load(placed("val%d" % t, 0, "val_pool%d" % t, [P, POOL], F32), rows_4p(vals)[:, t, :]))
         own_pairs = [load(tile("own_pair%d" % i, [P, 2, QUERIES], F32), rows_4p(own)[:, 2 * i:2 * i + 2, :])
                      for i in range(2)]
@@ -117,32 +117,55 @@ def tile_attend_ownlists_sinks_kernel(tc, query, keys, skey, size, ssz, vals, sv
             product(bank[:], columns(q_mx, j * P, (j + 1) * P), keys_mx, True, True)
             return bank
 
+        ssz_all = spread("ssz_all", ssz_col)
+        size_all = spread("size_all", size_col)
         key_planes = tile("key_planes", [P, PACK, SLOTS], BF16)
         for t in range(PACK):
             nc.vector.tensor_copy(out=key_planes[:, t, :], in_=key_pool[t][:].indirect(offsets[:]))
+        val_picked = [placed("picked2", 0, "val_picked%d" % t, [P, SLOTS], BF16) if t == 2
+                      else tile("val_picked%d" % t, [P, SLOTS], BF16) for t in range(PACK)]
+        for t in range(PACK):
+            nc.vector.tensor_copy(out=val_picked[t][:], in_=val_pool[t][:].indirect(offsets[:]))
 
         neg_max_b = tile("neg_max_b", [P, 2], F32)
         sum_b = tile("sum_b", [P, 2], F32)
         exp_b = tile("exp_b", [P, 2, SLOTS], F32)
+        weighted_b = tile("weighted_b", [P, 2, SLOTS], F32)
         for j in range(2):
             score = scores("score_b%d" % j, j, sk_mx, "acc%d" % j)
             nc.vector.tensor_reduce(out=neg_max_b[:, j:j + 1], in_=score[:], axis=AXIS_X, op=ALU.max, negate=True)
             nc.scalar.activation(out=exp_b[:, j, :], in_=score[:], func=EXP, bias=neg_max_b[:, j:j + 1],
                                  accum_out=sum_b[:, j:j + 1])
-        ssz_all = spread("ssz_all", ssz_col)
-        size_all = spread("size_all", size_col)
+        for j in range(2):
+            nc.vector.tensor_tensor(out=weighted_b[:, j, :], in0=exp_b[:, j, :], in1=ssz_all, op=ALU.mult)
 
         key_grouped = tile("key_grouped", [P, SLOTS, PACK], BF16)
         deal_on_both(key_grouped[:], key_planes[:])
-        key_mx = (tile("key_codes", [P, SLOTS], U32)[:], placed("small", 0, "key_scales", [P, SLOTS], U8)[:])
+        key_mx = mx_pair("key", SLOTS)
         quantise(key_mx, key_grouped[:].rearrange("p n t -> p (n t)"))
-        weighted_b = [placed("key3", 0, "weighted_b0", [P, SLOTS], F32)]
-        nc.vector.tensor_tensor(out=weighted_b[0][:], in0=exp_b[:, 0, :], in1=ssz_all, op=ALU.mult)
 
-        val_picked = [tile("val_picked%d" % t, [P, SLOTS], BF16) for t in range(PACK)]
-
-        def gather_values(t):
-            nc.vector.tensor_copy(out=val_picked[t][:], in_=val_pool[t][:].indirect(offsets[:]))
+        neg_a = placed("val0", 0, "neg_a", [P, 2, SLOTS], F32)
+        neg_max = tile("neg_max", [P, 2], F32)
+        sum_a = tile("sum_a", [P, 2], F32)
+        total = placed("total", 0, "total", [P, 2], F32)
+        exp_a = tile("exp_a", [P, 2, SLOTS], F32)
+        shift = tile("shift", [P, 2], F32)
+        for j in range(2):
+            score = scores("score_a%d" % j, j, key_mx, "acc%d" % (2 + j))
+            nc.vector.tensor_scalar(out=neg_a[:, j, :], in0=score[:], scalar1=-1.0, scalar2=neg_max_b[:, j:j + 1],
+                                    op0=ALU.mult, op1=ALU.min, accum_out=neg_max[:, j:j + 1])
+            nc.scalar.activation(out=exp_a[:, j, :], in_=neg_a[:, j, :], func=EXP, scale=-1.0,
+                                 bias=neg_max[:, j:j + 1], accum_out=sum_a[:, j:j + 1])
+            nc.scalar.activation(out=shift[:, j:j + 1], in_=neg_max_b[:, j:j + 1], func=EXP, scale=-1.0,
+                                 bias=neg_max[:, j:j + 1])
+        for j in range(2):
+            nc.scalar.activation(out=total[:, j:j + 1], in_=sum_b[:, j:j + 1], func=IDENTITY,
+                                 scale=shift[:, j:j + 1], bias=sum_a[:, j:j + 1])
+        inverse = tile("inverse", [P, 2], F32)
+        nc.vector.reciprocal(out=inverse[:], in_=total[:])
+        factor_b = tile("factor_b", [P, 2], F32)
+        for j in range(2):
+            nc.scalar.activation(out=factor_b[:, j:j + 1], in_=shift[:, j:j + 1], func=COPY, scale=inverse[:, j:j + 1])
 
         def turn_values(t, grouped):
             bank = ps.tile([P, 2, P], F32, name="bank_val%d" % t, tag="turn", bufs=4)
@@ -152,93 +175,82 @@ def tile_attend_ownlists_sinks_kernel(tc, query, keys, skey, size, ssz, vals, sv
             nc.scalar.copy(out=grouped.bitcast(F32).rearrange("p (n u) -> p n u", u=2),
                            in_=bank[:].rearrange("p u n -> p n u"))
 
-        gather_values(0)
-        neg_a = tile("neg_a", [P, 2, SLOTS], F32)
-        neg_max = tile("neg_max", [P, 2], F32)
-        sum_a = tile("sum_a", [P, 2], F32)
-        total = placed("small", 2048, "total", [P, 2], F32)
-        exp_a = tile("exp_a", [P, 2, SLOTS], F32)
-        shift = tile("shift", [P, 2], F32)
-        for j in range(2):
-            score = scores("score_a%d" % j, j, key_mx, "acc%d" % (2 + j))
-            nc.vector.tensor_scalar(out=neg_a[:, j, :], in0=score[:], scalar1=-1.0, scalar2=neg_max_b[:, j:j + 1],
-                                    op0=ALU.mult, op1=ALU.min, accum_out=neg_max[:, j:j + 1])
-            nc.scalar.activation(out=shift[:, j:j + 1], in_=neg_max_b[:, j:j + 1], func=EXP, scale=-1.0,
-                                 bias=neg_max[:, j:j + 1])
-            nc.scalar.activation(out=exp_a[:, j, :], in_=neg_a[:, j, :], func=EXP, scale=-1.0,
-                                 bias=neg_max[:, j:j + 1], accum_out=sum_a[:, j:j + 1])
-        for j in range(2):
-            nc.scalar.activation(out=total[:, j:j + 1], in_=sum_b[:, j:j + 1], func=IDENTITY,
-                                 scale=shift[:, j:j + 1], bias=sum_a[:, j:j + 1])
-        weighted_b.append(placed("small", 0, "weighted_b1", [P, SLOTS], F32))
-        nc.vector.tensor_tensor(out=weighted_b[1][:], in0=exp_b[:, 1, :], in1=ssz_all, op=ALU.mult)
-
-        def cast_sink_values(copy, grouped, pair, s):
-            copy(out=grouped[:].rearrange("p t s j -> p s j t")[:, s],
-                 in_=sv_raw[:].rearrange("p j (s t) -> p s j t", t=PACK)[:, s, :, 2 * pair:2 * pair + 2])
-
-        sv_grouped = [tile("sv_grouped0", [P, 2, P, PACK], BF16)]
-
-        gather_values(1)
-        inverse = placed("val1", 0, "inverse", [P, 2], F32)
-        nc.vector.reciprocal(out=inverse[:], in_=total[:])
-        factor_b = tile("factor_b", [P, 2], F32)
-        for j in range(2):
-            nc.scalar.activation(out=factor_b[:, j:j + 1], in_=shift[:, j:j + 1], func=COPY, scale=inverse[:, j:j + 1])
-        w_rows = [placed("small", 4096 + 2048 * a, "w_rows%d" % a, [P, 2, SLOTS], BF16) for a in range(2)]
-        for j in range(2):
-            nc.vector.scalar_tensor_tensor(out=w_rows[0][:, j, :], in0=exp_a[:, j, :], scalar=inverse[:, j:j + 1],
-                                           in1=size_all, op0=ALU.mult, op1=ALU.mult)
-            nc.scalar.activation(out=w_rows[1][:, j, :], in_=weighted_b[j][:], func=COPY, scale=factor_b[:, j:j + 1])
-        gather_values(2)
-        grouped01 = placed("small", 2048, "val_grouped01", [P, 2, SLOTS], BF16)
+        grouped01 = placed("total", 0, "val_grouped01", [P, 2, SLOTS], BF16)
         val_grouped = [tile("val_grouped%d" % t, [P, SLOTS], BF16) for t in range(2, PACK)]
         for t in range(2):
             turn_values(t, grouped01[:, t, :])
-        w_grouped = [tile("w_grouped%d" % a, [P, QUERIES * PACK], BF16) for a in range(2)]
-        for a in range(2):
+        w_rows = [tile("w_rows%d" % a, [P, 2, SLOTS], BF16) for a in range(2)]
+        for j in range(2):
+            nc.vector.scalar_tensor_tensor(out=w_rows[0][:, j, :], in0=exp_a[:, j, :], scalar=inverse[:, j:j + 1],
+                                           in1=size_all, op0=ALU.mult, op1=ALU.mult)
+            nc.scalar.activation(out=w_rows[1][:, j, :], in_=weighted_b[:, j, :], func=COPY, scale=factor_b[:, j:j + 1])
+
+        def turn_weights(a):
             bank = ps.tile([P, 2, 2, P], F32, name="bank_w%d" % a, tag="turn", bufs=4)
             words = w_rows[a][:].bitcast(F32)
             for j in range(2):
                 for u in range(2):
                     nc.tensor.transpose(bank[:, j, u, :], words[:, j, u * P:(u + 1) * P], ident[:])
-            nc.scalar.copy(out=w_grouped[a][:].bitcast(F32).rearrange("p (j n u) -> p j n u", j=2, u=2),
+            grouped = tile("w_grouped%d" % a, [P, QUERIES * PACK], BF16)
+            nc.scalar.copy(out=grouped[:].bitcast(F32).rearrange("p (j n u) -> p j n u", j=2, u=2),
                            in_=bank[:].rearrange("p j u n -> p j n u"))
-        for half in range(2):
-            cast_sink_values(nc.scalar.copy, sv_grouped[0], 0, slice(64 * half, 64 * half + 64))
-        turn_values(2, val_grouped[0][:])
-        gather_values(3)
-        turn_values(3, val_grouped[1][:])
-        sv_grouped.append(placed("small", 6144, "sv_grouped1", [P, 2, P, PACK], BF16))
-        for half in range(2):
-            cast_sink_values(nc.scalar.copy, sv_grouped[1], 1, slice(64 * half, 64 * half + 64))
+            return grouped
 
-        mx01 = mx_pair("val01", 2 * P, "val3", 0)
-        w_mx = [mx_pair("w0", QUERIES, "val3", 1024), mx_pair("w1", QUERIES, "val3", 2048)]
-        sv_mx = [mx_pair("sv%d" % i, 2 * P, "val3", 3072 + 1024 * i) for i in range(2)]
-        val_mx = [columns(mx01, 0, P), columns(mx01, P, 2 * P), mx_pair("val2", P, "val3", 5120), mx_pair("val3", P)]
+        def cast_sink_values(pair, grouped):
+            for half in range(2 - pair):
+                s = slice(64 * half, 64 * half + 64 * (1 + pair))
+                nc.scalar.copy(out=grouped[:].rearrange("p t s j -> p s j t")[:, s],
+                               in_=sv_raw[:].rearrange("p j (s t) -> p s j t", t=PACK)[:, s, :, 2 * pair:2 * pair + 2])
+            return grouped
+
+        w_grouped = [turn_weights(0)]
+        sv_grouped = [cast_sink_values(0, tile("sv_grouped0", [P, 2, P, PACK], BF16))]
+        w_grouped.append(turn_weights(1))
+        turn_values(2, val_grouped[0][:])
+        turn_values(3, val_grouped[1][:])
+        sv_grouped.append(cast_sink_values(1, placed("picked2", 0, "sv_grouped1", [P, 2, P, PACK], BF16)))
+        mx01 = mx_pair("val01", 2 * P)
+        w_mx = [mx_pair("w0", QUERIES, "val2", 0), mx_pair("w1", QUERIES, "val3", 1024)]
+        sv_mx = [mx_pair("sv%d" % i, 2 * P, "val3", 2048 + 1024 * i) for i in range(2)]
+        val_mx = [columns(mx01, 0, P), columns(mx01, P, 2 * P), mx_pair("val2", P, "val3", 0), mx_pair("val3", P)]
         quantise(mx01, grouped01[:].rearrange("p t n -> p (t n)"))
         quantise(w_mx[0], w_grouped[0][:])
         quantise(sv_mx[0], sv_grouped[0][:].rearrange("p t s j -> p (t s j)"))
         quantise(w_mx[1], w_grouped[1][:])
-        for t in range(2, PACK):
-            quantise(val_mx[t], val_grouped[t - 2][:])
-        quantise(sv_mx[1], sv_grouped[1][:].rearrange("p t s j -> p (t s j)"))
-
         result = tile("result", [P, PACK, PLACES], F32)
         masked = tile("masked", [P, PACK, QUERIES], F32)
         acc = [ps.tile([P, QUERIES], F32, name="acc_o%d" % t, tag="acc%d" % t) for t in range(PACK)]
-        for t in range(2):
+
+        def values_pass(t):
             product(acc[t][:], val_mx[t], w_mx[0], True, False)
-        for t in range(PACK):
-            if t >= 2:
-                product(acc[t][:], val_mx[t], w_mx[0], True, False)
+
+        def sinks_pass(t):
             product(acc[t][:], columns(sv_mx[t // 2], t % 2 * P, (t % 2 + 1) * P), w_mx[1], False, True)
-        for pair in range(2):
-            for t in (2 * pair, 2 * pair + 1):
-                nc.vector.tensor_tensor(out=masked[:, t, :], in0=acc[t][:], in1=own_pairs[pair][:, t % 2, :],
-                                        op=ALU.mult)
-            for t in (2 * pair, 2 * pair + 1):
-                nc.vector.tensor_reduce(out=result[:, t, :], in_=masked[:, t, :].rearrange("p (x h) -> p x h", h=HEADS),
-                                        axis=AXIS_X, op=ALU.add)
+
+        def mask(t):
+            nc.vector.tensor_tensor(out=masked[:, t, :], in0=acc[t][:], in1=own_pairs[t // 2][:, t % 2, :], op=ALU.mult)
+
+        def add_heads(first, last):
+            nc.vector.tensor_reduce(out=result[:, first:last, :],
+                                    in_=masked[:, first:last, :].rearrange("p t (x h) -> p t x h", h=HEADS),
+                                    axis=AXIS_X, op=ALU.add)
+
+        for t in range(2):
+            values_pass(t)
+        for t in range(2):
+            sinks_pass(t)
+        quantise(val_mx[2], val_grouped[0][:])
+        values_pass(2)
+        quantise(sv_mx[1], sv_grouped[1][:].rearrange("p t s j -> p (t s j)"))
+        quantise(val_mx[3], val_grouped[1][:])
+        values_pass(3)
+        sinks_pass(2)
+        sinks_pass(3)
+        mask(0)
+        mask(1)
+        mask(2)
+        add_heads(0, 2)
+        mask(3)
+        add_heads(2, 3)
+        add_heads(3, 4)
         nc.sync.dma_start(out=rows_4p(out), in_=result[:])

from contextlib import ExitStack

import concourse.mybir as mybir
from concourse.masks import make_identity

F32 = mybir.dt.float32
BF16 = mybir.dt.bfloat16
U32 = mybir.dt.uint32
U16 = mybir.dt.uint16
U8 = mybir.dt.uint8
FP8X4 = mybir.dt.float8_e4m3fn_x4
ALU = mybir.AluOpType
EXP = mybir.ActivationFunctionType.Exp
IDENTITY = mybir.ActivationFunctionType.Identity
COPY = mybir.ActivationFunctionType.Copy
AXIS_X = mybir.AxisListType.X

P = 128
PACK = 4
POOL = 2048
SLOTS = 512
QUERIES = 256
PLACES = 32
HEADS = 8
KEY_SPLIT = 84
REGION = 8192
REGIONS = ("val0", "val2", "val3", "total", "picked2")
FLOPS = 4 * 2 * 512 * 512 * 256


def tile_attend_ownlists_sinks_kernel(tc, query, keys, skey, size, ssz, vals, sval, own, offs, out):
    nc = tc.nc
    with ExitStack() as ctx:
        sb = ctx.enter_context(tc.tile_pool(name="sb", bufs=1))
        shared = ctx.enter_context(tc.tile_pool(name="shared", bufs=1))
        ps = ctx.enter_context(tc.psum_pool(name="ps", bufs=1))

        def tile(name, shape, dtype):
            return sb.tile(shape, dtype, name=name, align_bytes=64)

        def placed(region, start, name, shape, dtype):
            return shared.tile(shape, dtype, name=name, align_bytes=64, offset=REGIONS.index(region) * REGION + start)

        def load(dst, src):
            nc.sync.dma_start(out=dst[:], in_=src)
            return dst

        def quantise(pair, grouped):
            nc.vector.quantize_mx(out=pair[0].bitcast(FP8X4), scales=pair[1], in_=grouped)

        def product(acc, lhs, rhs, start, stop):
            nc.tensor.matmul_mx(out=acc, lhsT=lhs[0].bitcast(FP8X4), lhsT_scale=lhs[1],
                                rhs=rhs[0].bitcast(FP8X4), rhs_scale=rhs[1], start=start, stop=stop)

        def interleave(copy, dst, src):
            copy(out=dst.rearrange("p (c i) t -> p c t i", i=4), in_=src.rearrange("p t (c i) -> p c t i", i=4))

        def deal(copy, dst, src, places):
            copy(out=dst.rearrange("p (u s e) t -> p s t u e", u=2, e=2)[:, places],
                 in_=src.rearrange("p t (s u e) -> p s t u e", u=2, e=2)[:, places])

        def rows_4p(src):
            return src.rearrange("(p t) n -> p t n", t=PACK)

        def columns(pair, start, stop):
            return (pair[0][:, start:stop], pair[1][:, start:stop])

        def mx_pair(name, width, region=None, start=0):
            codes = tile(name + "_codes", [P, width], U32) if region is None else placed(
                region, start, name + "_codes", [P, width], U32)
            return (codes[:], tile(name + "_scales", [P, width], U8)[:])

        offsets = sb.tile([P, SLOTS // 16], U16, name="offsets")
        ssz_col = tile("ssz_col", [P, PACK], F32)
        size_col = tile("size_col", [P, PACK], F32)
        nc.scalar.dma_start(out=ssz_col[:], in_=ssz.rearrange("o (p c) -> (o p) c", c=PACK))
        nc.scalar.dma_start(out=size_col[:], in_=size.rearrange("o (p c) -> (o p) c", c=PACK))
        q_raw = load(tile("q_raw", [P, PACK, QUERIES], F32), rows_4p(query))
        sk_raw = load(tile("sk_raw", [P, PACK, SLOTS], F32), rows_4p(skey))
        nc.sync.dma_start(offsets[:], offs)
        key_pool = [load(tile("key_pool%d" % t, [P, POOL], F32), rows_4p(keys)[:, t, :]) for t in range(PACK)]
        val_pool = [load(placed("val0", 0, "val_pool0", [P, POOL], F32), rows_4p(vals)[:, 0, :]),
                    load(tile("val_pool1", [P, POOL], F32), rows_4p(vals)[:, 1, :])]
        sv_raw = load(tile("sv_raw", [P, PACK, SLOTS], F32), rows_4p(sval))
        for t in range(2, PACK):
            val_pool.append(load(placed("val%d" % t, 0, "val_pool%d" % t, [P, POOL], F32), rows_4p(vals)[:, t, :]))
        own_pairs = [load(tile("own_pair%d" % i, [P, 2, QUERIES], F32), rows_4p(own)[:, 2 * i:2 * i + 2, :])
                     for i in range(2)]

        ident = tile("ident", [P, P], F32)
        make_identity(nc, ident[:])

        def deal_on_both(dst, src):
            deal(nc.vector.tensor_copy, dst, src, slice(0, KEY_SPLIT))
            deal(nc.scalar.copy, dst, src, slice(KEY_SPLIT, P))

        q_grouped = tile("q_grouped", [P, QUERIES, PACK], BF16)
        interleave(nc.vector.tensor_copy, q_grouped[:], q_raw[:])
        q_mx = mx_pair("q", QUERIES)
        quantise(q_mx, q_grouped[:].rearrange("p n t -> p (n t)"))
        sk_grouped = tile("sk_grouped", [P, SLOTS, PACK], BF16)
        deal_on_both(sk_grouped[:], sk_raw[:])
        sk_mx = mx_pair("sk", SLOTS)
        quantise(sk_mx, sk_grouped[:].rearrange("p n t -> p (n t)"))

        def spread(name, col):
            bank = ps.tile([P, PACK, P], F32, name="bank_" + name, tag="turn", bufs=4)
            for c in range(PACK):
                nc.tensor.transpose(bank[:, c, :], col[:, c:c + 1].to_broadcast([P, P]), ident[:])
            row = tile(name, [P, SLOTS], F32)
            nc.scalar.copy(out=row[:].rearrange("p (u s e) -> p u s e", u=2, e=2),
                           in_=bank[:].rearrange("p (u e) s -> p u s e", u=2))
            return row[:]

        def scores(name, j, keys_mx, tag):
            bank = ps.tile([P, SLOTS], F32, name=name, tag=tag)
            product(bank[:], columns(q_mx, j * P, (j + 1) * P), keys_mx, True, True)
            return bank

        ssz_all = spread("ssz_all", ssz_col)
        size_all = spread("size_all", size_col)
        key_planes = tile("key_planes", [P, PACK, SLOTS], BF16)
        for t in range(PACK):
            nc.vector.tensor_copy(out=key_planes[:, t, :], in_=key_pool[t][:].indirect(offsets[:]))
        val_picked = [placed("picked2", 0, "val_picked%d" % t, [P, SLOTS], BF16) if t == 2
                      else tile("val_picked%d" % t, [P, SLOTS], BF16) for t in range(PACK)]
        for t in range(PACK):
            nc.vector.tensor_copy(out=val_picked[t][:], in_=val_pool[t][:].indirect(offsets[:]))

        neg_max_b = tile("neg_max_b", [P, 2], F32)
        sum_b = tile("sum_b", [P, 2], F32)
        exp_b = tile("exp_b", [P, 2, SLOTS], F32)
        weighted_b = tile("weighted_b", [P, 2, SLOTS], F32)
        for j in range(2):
            score = scores("score_b%d" % j, j, sk_mx, "acc%d" % j)
            nc.vector.tensor_reduce(out=neg_max_b[:, j:j + 1], in_=score[:], axis=AXIS_X, op=ALU.max, negate=True)
            nc.scalar.activation(out=exp_b[:, j, :], in_=score[:], func=EXP, bias=neg_max_b[:, j:j + 1],
                                 accum_out=sum_b[:, j:j + 1])
        for j in range(2):
            nc.vector.tensor_tensor(out=weighted_b[:, j, :], in0=exp_b[:, j, :], in1=ssz_all, op=ALU.mult)

        key_grouped = tile("key_grouped", [P, SLOTS, PACK], BF16)
        deal_on_both(key_grouped[:], key_planes[:])
        key_mx = mx_pair("key", SLOTS)
        quantise(key_mx, key_grouped[:].rearrange("p n t -> p (n t)"))

        neg_a = placed("val0", 0, "neg_a", [P, 2, SLOTS], F32)
        neg_max = tile("neg_max", [P, 2], F32)
        sum_a = tile("sum_a", [P, 2], F32)
        total = placed("total", 0, "total", [P, 2], F32)
        exp_a = tile("exp_a", [P, 2, SLOTS], F32)
        shift = tile("shift", [P, 2], F32)
        for j in range(2):
            score = scores("score_a%d" % j, j, key_mx, "acc%d" % (2 + j))
            nc.vector.tensor_scalar(out=neg_a[:, j, :], in0=score[:], scalar1=-1.0, scalar2=neg_max_b[:, j:j + 1],
                                    op0=ALU.mult, op1=ALU.min, accum_out=neg_max[:, j:j + 1])
            nc.scalar.activation(out=exp_a[:, j, :], in_=neg_a[:, j, :], func=EXP, scale=-1.0,
                                 bias=neg_max[:, j:j + 1], accum_out=sum_a[:, j:j + 1])
            nc.scalar.activation(out=shift[:, j:j + 1], in_=neg_max_b[:, j:j + 1], func=EXP, scale=-1.0,
                                 bias=neg_max[:, j:j + 1])
        for j in range(2):
            nc.scalar.activation(out=total[:, j:j + 1], in_=sum_b[:, j:j + 1], func=IDENTITY,
                                 scale=shift[:, j:j + 1], bias=sum_a[:, j:j + 1])
        inverse = tile("inverse", [P, 2], F32)
        nc.vector.reciprocal(out=inverse[:], in_=total[:])
        factor_b = tile("factor_b", [P, 2], F32)
        for j in range(2):
            nc.scalar.activation(out=factor_b[:, j:j + 1], in_=shift[:, j:j + 1], func=COPY, scale=inverse[:, j:j + 1])

        def turn_values(t, grouped):
            bank = ps.tile([P, 2, P], F32, name="bank_val%d" % t, tag="turn", bufs=4)
            words = val_picked[t][:].bitcast(F32)
            for u in range(2):
                nc.tensor.transpose(bank[:, u, :], words[:, u::2], ident[:])
            nc.scalar.copy(out=grouped.bitcast(F32).rearrange("p (n u) -> p n u", u=2),
                           in_=bank[:].rearrange("p u n -> p n u"))

        grouped01 = placed("total", 0, "val_grouped01", [P, 2, SLOTS], BF16)
        val_grouped = [tile("val_grouped%d" % t, [P, SLOTS], BF16) for t in range(2, PACK)]
        for t in range(2):
            turn_values(t, grouped01[:, t, :])
        w_rows = [tile("w_rows%d" % a, [P, 2, SLOTS], BF16) for a in range(2)]
        for j in range(2):
            nc.vector.scalar_tensor_tensor(out=w_rows[0][:, j, :], in0=exp_a[:, j, :], scalar=inverse[:, j:j + 1],
                                           in1=size_all, op0=ALU.mult, op1=ALU.mult)
            nc.scalar.activation(out=w_rows[1][:, j, :], in_=weighted_b[:, j, :], func=COPY, scale=factor_b[:, j:j + 1])

        def turn_weights(a):
            bank = ps.tile([P, 2, 2, P], F32, name="bank_w%d" % a, tag="turn", bufs=4)
            words = w_rows[a][:].bitcast(F32)
            for j in range(2):
                for u in range(2):
                    nc.tensor.transpose(bank[:, j, u, :], words[:, j, u * P:(u + 1) * P], ident[:])
            grouped = tile("w_grouped%d" % a, [P, QUERIES * PACK], BF16)
            nc.scalar.copy(out=grouped[:].bitcast(F32).rearrange("p (j n u) -> p j n u", j=2, u=2),
                           in_=bank[:].rearrange("p j u n -> p j n u"))
            return grouped

        def cast_sink_values(pair, grouped):
            for half in range(2 - pair):
                s = slice(64 * half, 64 * half + 64 * (1 + pair))
                nc.scalar.copy(out=grouped[:].rearrange("p t s j -> p s j t")[:, s],
                               in_=sv_raw[:].rearrange("p j (s t) -> p s j t", t=PACK)[:, s, :, 2 * pair:2 * pair + 2])
            return grouped

        w_grouped = [turn_weights(0)]
        sv_grouped = [cast_sink_values(0, tile("sv_grouped0", [P, 2, P, PACK], BF16))]
        w_grouped.append(turn_weights(1))
        turn_values(2, val_grouped[0][:])
        turn_values(3, val_grouped[1][:])
        sv_grouped.append(cast_sink_values(1, placed("picked2", 0, "sv_grouped1", [P, 2, P, PACK], BF16)))
        mx01 = mx_pair("val01", 2 * P)
        w_mx = [mx_pair("w0", QUERIES, "val2", 0), mx_pair("w1", QUERIES, "val3", 1024)]
        sv_mx = [mx_pair("sv%d" % i, 2 * P, "val3", 2048 + 1024 * i) for i in range(2)]
        val_mx = [columns(mx01, 0, P), columns(mx01, P, 2 * P), mx_pair("val2", P, "val3", 0), mx_pair("val3", P)]
        quantise(mx01, grouped01[:].rearrange("p t n -> p (t n)"))
        quantise(w_mx[0], w_grouped[0][:])
        quantise(sv_mx[0], sv_grouped[0][:].rearrange("p t s j -> p (t s j)"))
        quantise(w_mx[1], w_grouped[1][:])
        result = tile("result", [P, PACK, PLACES], F32)
        masked = tile("masked", [P, PACK, QUERIES], F32)
        acc = [ps.tile([P, QUERIES], F32, name="acc_o%d" % t, tag="acc%d" % t) for t in range(PACK)]

        def values_pass(t):
            product(acc[t][:], val_mx[t], w_mx[0], True, False)

        def sinks_pass(t):
            product(acc[t][:], columns(sv_mx[t // 2], t % 2 * P, (t % 2 + 1) * P), w_mx[1], False, True)

        def mask(t):
            nc.vector.tensor_tensor(out=masked[:, t, :], in0=acc[t][:], in1=own_pairs[t // 2][:, t % 2, :], op=ALU.mult)

        def add_heads(first, last):
            nc.vector.tensor_reduce(out=result[:, first:last, :],
                                    in_=masked[:, first:last, :].rearrange("p t (x h) -> p t x h", h=HEADS),
                                    axis=AXIS_X, op=ALU.add)

        for t in range(2):
            values_pass(t)
        for t in range(2):
            sinks_pass(t)
        quantise(val_mx[2], val_grouped[0][:])
        values_pass(2)
        quantise(sv_mx[1], sv_grouped[1][:].rearrange("p t s j -> p (t s j)"))
        quantise(val_mx[3], val_grouped[1][:])
        values_pass(3)
        sinks_pass(2)
        sinks_pass(3)
        mask(0)
        mask(1)
        mask(2)
        add_heads(0, 2)
        mask(3)
        add_heads(2, 3)
        add_heads(3, 4)
        nc.sync.dma_start(out=rows_4p(out), in_=result[:])
